import numpy as np, ml_dtypes
CORES = [2,6,10,14,18,22,26,30]
N = 8
BF = ml_dtypes.bfloat16
def gentries(a):
    return np.ascontiguousarray(a.reshape(8, 16, -1).transpose(0, 2, 1)).reshape(8, -1)
def gtable(e):
    e = np.asarray(e); return np.ascontiguousarray(e.reshape(8, -1, 16).transpose(0, 2, 1)).reshape(128, -1).astype(np.int32)
def f(rng, *shape):
    return (rng.standard_normal(shape, dtype=np.float32) * np.exp2(rng.integers(-2, 3, shape[:-1] + (1,)))).astype(BF)
def wide(rng, *shape):
    v = f(rng, *shape).astype(np.float32); k = shape[:-2] + (1, shape[-1])
    return (v * np.exp2(rng.integers(-6, 7, k)) * (rng.random(k) > 0.0625)).astype(BF)
P, E, M, G = 2048, 4096, 512, 128
Z = P + (N - 1) * G
DX, DY = (-1, 0, 1, -1, 1, -1, 0, 1), (-1, -1, -1, 0, 0, 1, 1, 1)
FAR = [[(d, s) for d in range(8) for s in range(4) if max(abs(2 * DX[d] + s % 2 - c % 2), abs(2 * DY[d] + s // 2 - c // 2)) > 1] for c in range(4)]
def kids(rng):
    return rng.permuted(np.tile(np.minimum(np.arange(4 * P), E), (N, 8, 1)), axis=2).reshape(N, 8, 4, P)
def nears(rng, own, ghost):
    u = rng.random((N, 8, 8, M))
    return np.where(u < own, rng.integers(0, P, u.shape), np.where(u < own + ghost, rng.integers(P, Z, u.shape), Z))
def gives(rng):
    return rng.integers(0, P, (N, 8, N - 1, G))
def pack(rng, ki, ne, gi):
    return {"ex": f(rng, N, 128, E), "kid": ki.reshape(N, 8, 4 * P).astype(np.int32), "near": np.stack([gtable(a.reshape(8, 8 * M)) for a in ne]),
            "give": np.stack([gtable(a.reshape(8, (N - 1) * G)) for a in gi]), "tr": f(rng, N, 128, 108)}
def setup_inputs(rng):
    return pack(rng, kids(rng), nears(rng, 0.5, 0.42), gives(rng))
def setup_inputs_ghosts(rng):
    ne = nears(rng, 0.0, 2.0); q = rng.integers(0, N); ne[q] = P + G * rng.integers(0, N - 1) + rng.integers(0, G, (8, 8, M))
    for b in range(N - 1):
        ne[:, :, b, 0] = P + G * b; ne[:, :, b, M - 1] = P + G * b + G - 1
    return pack(rng, kids(rng), ne, gives(rng))
def setup_inputs_empty(rng):
    ne = nears(rng, 0.15, 0.15); ne[:, :, :, ::4] = Z; ne[:, rng.choice(np.array([0, 3, 4, 6, 7]))] = Z
    ki = kids(rng); ki[:, :, :, rng.random(P) < 0.5] = E; b = rng.integers(0, P)
    ki[:, :, :, b] = rng.integers(0, E, (N, 8, 4)); ne[:, 1:3, 0, 1] = b
    ne[:, 5, 7, 2] = b
    return pack(rng, ki, ne, gives(rng))
def setup_inputs_ends(rng):
    ne = rng.choice(np.array([0, P - 1, P, P + G - 1, Z - G, Z - 1, Z]), (N, 8, 8, M)); ki = kids(rng)
    for p in (0, P - 1): ki[:, :, :, p] = rng.permuted(np.tile(np.array([0, E - 1, E, E - 1]), (N, 8, 1)), axis=2)
    return pack(rng, ki, ne, rng.choice(np.array([0, P - 1]), (N, 8, N - 1, G)))
def setup_inputs_alike(rng):
    ne = np.tile(rng.integers(0, Z, (N, 8, 8, 1)), (1, 1, 1, M)); gi = np.tile(rng.integers(0, P, (N, 8, N - 1, 1)), (1, 1, 1, G))
    return pack(rng, rng.integers(0, E, (N, 8, 4, P)), ne, gi)
def setup_inputs_spread(rng):
    d = setup_inputs(rng); d["ex"] = wide(rng, N, 128, E); return d
def check_inputs(d):
    bad = []
    for a, top in (("kid", E), ("near", Z), ("give", P - 1)):
        if d[a].min() < 0 or d[a].max() > top: bad.append(a)
    for a in ("ex", "tr"):
        if not np.isfinite(d[a].astype(np.float32)).all(): bad.append(a)
    return bad
def reference(ex, kid, near, give, tr):
    x = np.concatenate([ex.astype(np.float64).reshape(N, 8, 16, E), np.zeros((N, 8, 16, 1))], 3)
    ch = kid.reshape(N, 8, 4, P); t = tr.astype(np.float64).reshape(N, 8, 16, 4, 27)
    gi = [gentries(a).reshape(8, N - 1, G) for a in give]; ne = [gentries(a).reshape(8, 8, M) for a in near]
    y = np.zeros((N, 8, 16, 4, M), np.float64)
    for r in range(N):
        for g in range(8):
            w = [x[r, g][:, ch[r, g]]]
            for d in range(1, N):
                q = (r - d) % N
                w.append(x[q, g][:, ch[q, g][:, gi[q][g, d - 1]]])
            w = np.concatenate(w + [np.zeros((16, 4, 1))], 2)
            v = w[:, :, ne[r][g]]
            for c in range(4):
                for i, (d, s) in enumerate(FAR[c]):
                    y[r, g, :, c] += t[r, g, :, c, i, None] * v[:, s, d]
    return {"y": y.reshape(N, 128, 4 * M).astype(np.float32)}

@@ -1,0 +1,303 @@
+import numpy as np
+from concourse.bass import DstId, RemoteDMATransfer
+from concourse.mybir import dt, AluOpType, AxisListType, ActivationFunctionType
+
+OP = AluOpType
+COPY = ActivationFunctionType.Copy
+N, P, E, M, G = 8, 2048, 4096, 512, 128
+DX, DY = (-1, 0, 1, -1, 1, -1, 0, 1), (-1, -1, -1, 0, 0, 1, 1, 1)
+FAR = [[(d, s) for d in range(8) for s in range(4)
+        if max(abs(2 * DX[d] + s % 2 - c % 2), abs(2 * DY[d] + s // 2 - c // 2)) > 1] for c in range(4)]
+XW = E + 16
+GW = 2 * (N - 1) * G
+TW = 2 * P + GW + 16
+
+SCRATCH = {
+    "kl": ("sbuf", [128, 512], "int32"), "ku": ("sbuf", [128, 512], "uint16"),
+    "ni": ("sbuf", [128, 256], "int32"), "gi": ("sbuf", [128, 56], "int32"),
+    "nf": ("sbuf", [128, 256], "float32"), "gf": ("sbuf", [128, 56], "float32"),
+    "nu": ("sbuf", [128, 1024], "uint16"), "gu": ("sbuf", [128, 224], "uint16"),
+    "im": ("sbuf", [128, 128], "int32"), "im2": ("sbuf", [128, 128], "int32"),
+    "ip": ("sbuf", [128, 8], "int32"), "ip2": ("sbuf", [128, 8], "int32"), "cc": ("sbuf", [128, 8], "float32"),
+    "rm": ("sbuf", [128, 128], "float32"), "em": ("sbuf", [128, 224], "bfloat16"),
+    "tri": ("sbuf", [128, 108], "bfloat16"), "trf": ("sbuf", [128, 128], "bfloat16"),
+    "trr": ("sbuf", [128, 128], "bfloat16"), "lt": ("sbuf", [128, 4096], "bfloat16"),
+    "o": ("sbuf", [128, 2048], "float32"),
+    "psy": ("psum", [128, 2048], "float32"), "psa": ("psum", [128, 2048], "float32"),
+}
+for _k in range(4):
+    SCRATCH["xr%d" % _k] = ("sbuf", [128, XW], "bfloat16")
+    SCRATCH["v%d" % _k] = ("sbuf", [128, 8 * M], "bfloat16")
+for _h in range(2):
+    SCRATCH["tab%d" % _h] = ("sbuf", [128, TW], "bfloat16")
+    SCRATCH["gb%d" % _h] = ("sbuf", [128, GW], "bfloat16")
+for _n in range(6):
+    SCRATCH["na%d" % _n] = ("sbuf", [128, 256], "int32")
+for _n in range(3):
+    SCRATCH["ga%d" % _n] = ("sbuf", [128, 56], "int32")
+SEMAPHORES = (["sv", "ss", "sp", "sg", "sent", "arr0", "arr1", "dg", "dn", "dt", "dy"]
+              + ["dk%d" % k for k in range(4)] + ["dx%d" % k for k in range(4)])
+
+
+def sends(q, cores, topo):
+    me = cores[q]
+    kinds = {"chip": [], "mate": [], "plane": [], "far": []}
+    for d in range(1, N):
+        c = cores[(q + d) % N]
+        a, b = topo.chip(me), topo.chip(c)
+        kinds["chip" if a == b else "mate" if topo.mates(a, b) else "plane" if topo.same_plane(a, b) else "far"].append((d, c))
+    first = kinds["far"] + kinds["mate"][:1] + kinds["plane"][:1]
+    second = kinds["mate"][1:] + kinds["plane"][1:]
+    calls = []
+    for group in (first, second):
+        call = []
+        for j, (d, c) in enumerate(group):
+            eng = topo.engines(me, c)
+            n = len(eng) // len(group)
+            call.append((d, c, eng[n * j:n * j + n]))
+        calls.append(call)
+    used = set(topo.engines(me, first[0][1]))
+    for d, c in kinds["chip"]:
+        calls[1].append((d, c, [e for e in topo.engines(me, c) if e not in used]))
+    return calls
+
+
+def rank_program(g, core, T, topo):
+    rank = T.rank_of(core)
+    if rank is None:
+        return
+    cores = list(T.cores)
+    V, S, PE, SY = g.vector, g.scalar, g.tensor, g.sync
+    cnt = {"sv": 0, "ss": 0, "sp": 0, "sg": 0}
+    seen = {}
+
+    def inc(name, op):
+        op.then_inc(T.sem[name], 1)
+        cnt[name] += 1
+        return cnt[name]
+
+    def wait(qn, q, name, n):
+        if seen.get((qn, name), 0) < n:
+            q.wait_ge(T.sem[name], n)
+            seen[(qn, name)] = n
+
+    def vw(name, n):
+        wait("V", V, name, n)
+
+    def sw(name, n):
+        wait("S", S, name, n)
+
+    def pw(name, n):
+        wait("P", PE, name, n)
+
+    def load_k(q, k):
+        for s in range(4):
+            q.dma_start(T.kl[32 * s:32 * s + 32, 128 * k:128 * k + 128],
+                        T.kid[2 * k:2 * k + 2, P * s:P * s + P]).then_inc(T.sem["dk%d" % k], 16)
+
+    def load_x(q, k, ss):
+        for s in ss:
+            q.dma_start(T["xr%d" % k][32 * s:32 * s + 32, 0:E], T.ex[32 * k:32 * k + 32, :]).then_inc(T.sem["dx%d" % k], 16)
+
+    S.dma_start(T.gi[:], T.give[:]).then_inc(T.sem.dg, 16)
+    S.dma_start(T.ni[:], T.near[:]).then_inc(T.sem.dn, 16)
+    load_k(SY, 0)
+    load_x(SY, 0, (0, 1))
+    load_x(S, 0, (2, 3))
+    S.dma_start(T.tri[:], T.tr[:]).then_inc(T.sem.dt, 16)
+    load_k(SY, 1)
+    load_x(SY, 1, (0, 1))
+    load_x(S, 1, (2, 3))
+    for k in (2, 3):
+        load_k(SY, k)
+        load_x(SY, k, (0, 1, 2, 3))
+
+    i1 = inc("sg", g.iota(T.im[:], [[-1, 128]], 128, 1))
+    i2 = inc("sg", g.iota(T.ip[:], [[0, 8]], 0, 1))
+    m_trf = inc("sv", V.memset(T.trf[:], 0.0))
+    for k in range(4):
+        m_x = inc("sv", V.memset(T["xr%d" % k][:, E:XW], 0.0))
+    for h in range(2):
+        m_t = inc("sv", V.memset(T["tab%d" % h][:, 2 * P + GW:TW], 0.0))
+    m_em = inc("sv", V.memset(T.em[:], 0.0))
+    vw("sg", i2)
+    a = inc("sv", V.tensor_scalar(T.im2[:], T.im[:], 31, None, OP.bitwise_and))
+    b = inc("sv", V.tensor_scalar(T.ip2[:], T.ip[:], 5, 1, OP.arith_shift_right, OP.bitwise_and))
+    vw("sv", a)
+    v_rm = inc("sv", V.tensor_scalar(T.rm[:], T.im2[:], 0, None, OP.is_equal))
+    vw("sv", b)
+    v_cc = inc("sv", V.tensor_scalar(T.cc[:], T.ip2[:], -2047, 2047, OP.mult, OP.add))
+    vw("sv", v_rm)
+    v_em = inc("sv", V.tensor_copy(T.em[:, 96:128], T.rm[:, 0:32]))
+
+    sw("dt", 16)
+    sw("sv", m_trf)
+    for c in range(4):
+        pos = [4 * d + s for d, s in FAR[c]]
+        i = 0
+        while i < 27:
+            j = i
+            while j + 1 < 27 and pos[j + 1] == pos[j] + 1:
+                j += 1
+            s_trf = inc("ss", S.activation(T.trf[:, 32 * c + pos[i]:32 * c + pos[j] + 1],
+                                           T.tri[:, 27 * c + i:27 * c + j + 1], COPY))
+            i = j + 1
+
+    vw("dg", 16)
+    g1 = inc("sv", V.tensor_scalar(T.ga0[:], T.gi[:], 16, None, OP.mult))
+    g2 = inc("sv", V.tensor_scalar(T.ga1[:], T.gi[:], 7, None, OP.arith_shift_right))
+    vw("dn", 16)
+    n1 = inc("sv", V.tensor_scalar(T.na0[:], T.ni[:], P - 1, 16, OP.min, OP.mult))
+    vw("sv", g2)
+    g3 = inc("sv", V.tensor_scalar(T.ga2[:], T.ga1[:], -2047, None, OP.mult))
+    n3 = inc("sv", V.tensor_scalar(T.na2[:], T.ni[:], P - 1, 2, OP.max, OP.mult))
+    vw("sv", g3)
+    g4 = inc("sv", V.tensor_tensor(T.gf[:], T.ga0[:], T.ga2[:], OP.add))
+    n2 = inc("sv", V.tensor_scalar(T.na1[:], T.na0[:], 11, None, OP.arith_shift_right))
+    n4 = inc("sv", V.tensor_scalar(T.na3[:], T.ni[:], P, T.cc[:, 0:1], OP.is_ge, OP.mult))
+    vw("sv", n2)
+    n5 = inc("sv", V.tensor_scalar(T.na4[:], T.na1[:], -2047, -4094, OP.mult, OP.add))
+    vw("dk0", 64)
+    v_ku = [inc("sv", V.tensor_copy(T.ku[:, 0:128], T.kl[:, 0:128]))]
+    pw("sv", g4)
+    for k in range(4):
+        p_g = inc("sp", PE.matmul(T.psy[:, 512 * k:512 * k + 56], T.rm[32 * k:32 * k + 32, :], T.gf[32 * k:32 * k + 32, :], True, True))
+    vw("sp", p_g)
+    for k in range(4):
+        v_gu = inc("sv", V.tensor_copy(T.gu[:, 56 * k:56 * k + 56], T.psy[:, 512 * k:512 * k + 56]))
+    vw("sv", n4)
+    n6 = inc("sv", V.tensor_tensor(T.na5[:], T.na0[:], T.na2[:], OP.add))
+    vw("sv", n5)
+    n7 = inc("sv", V.tensor_tensor(T.na1[:], T.na3[:], T.na4[:], OP.add))
+    vw("sv", n7)
+    n8 = inc("sv", V.tensor_tensor(T.nf[:], T.na5[:], T.na1[:], OP.add))
+    pw("ss", s_trf)
+    pw("sv", max(v_em, v_gu))
+    for k in range(4):
+        for s in range(4):
+            op = PE.matmul(T.psy[:, 512 * k:512 * k + 32], T.em[32 * k:32 * k + 32, 96 - 32 * s:224 - 32 * s],
+                           T.trf[32 * k:32 * k + 32, s::4], s == 0, s == 3)
+            p_t = inc("sp", op)
+    pw("sv", n8)
+    for k in range(4):
+        p_n = inc("sp", PE.matmul(T.psa[:, 512 * k:512 * k + 256], T.rm[32 * k:32 * k + 32, :], T.nf[32 * k:32 * k + 32, :], True, True))
+
+    VC, GC = 64, 28
+    done = {}
+
+    def level1(k):
+        h, j = k // 2, k % 2
+        x, t = T["xr%d" % k], T["tab%d" % h]
+        vw("dx%d" % k, 64)
+        vw("sv", max(v_ku[k], m_x))
+        lv = inc("sv", V.tensor_copy(t[:, P * j:P * j + 16 * VC], x[:, 0:XW].indirect(T.ku[:, 128 * k:128 * k + VC])))
+        sw("dx%d" % k, 64)
+        sw("sv", max(v_ku[k], m_x))
+        ls = inc("ss", S.activation(t[:, P * j + 16 * VC:P * j + P], x[:, 0:XW].indirect(T.ku[:, 128 * k + VC:128 * k + 128]), COPY))
+        done[k] = (lv, ls)
+
+    def conv(k):
+        vw("dk%d" % k, 64)
+        v_ku.append(inc("sv", V.tensor_copy(T.ku[:, 128 * k:128 * k + 128], T.kl[:, 128 * k:128 * k + 128])))
+
+    def ghosts(k):
+        h, j = k // 2, k % 2
+        t, b = T["tab%d" % h], T["gb%d" % h]
+        lv, ls = done[k]
+        w = t[:, P * j:P * j + P]
+        vw("sv", max(lv, v_gu))
+        vw("ss", ls)
+        gv = inc("sv", V.tensor_copy(b[:, j:32 * GC:2], w.indirect(T.gu[:, 56 * k:56 * k + GC])))
+        sw("ss", ls)
+        sw("sv", max(lv, v_gu))
+        gs = inc("ss", S.activation(b[:, 32 * GC + j:GW:2], w.indirect(T.gu[:, 56 * k + GC:56 * k + 56]), COPY))
+        return gv, gs
+
+    plan = sends(rank, cores, topo)
+    sent = 0
+    for h in range(2):
+        for k in (2 * h, 2 * h + 1):
+            if k:
+                conv(k)
+            level1(k)
+            gv, gs = ghosts(k)
+        g.wait_ge(T.sem.sv, gv)
+        g.wait_ge(T.sem.ss, gs)
+        b, t = T["gb%d" % h], T["tab%d" % h]
+        for call in plan:
+            tr = []
+            for d, c, eng in call:
+                ad = topo.addr(c)
+                lo = 2 * G * (d - 1)
+                tr.append(RemoteDMATransfer(dst_ids=[DstId(rid=ad[0], pnc=ad[1])], dma_engine_mask=sum(1 << e for e in eng),
+                                            remote_sem=T.sem["arr%d" % h], src=b[:, lo:lo + 2 * G],
+                                            dst=t[:, 2 * P + lo:2 * P + lo + 2 * G]))
+                sent += len(eng)
+            g.remote_dma_fused(tr, local_sem=T.sem.sent)
+
+    vw("sp", p_t)
+    for k in range(4):
+        v_trr = inc("sv", V.tensor_copy(T.trr[:, k::4], T.psy[:, 512 * k:512 * k + 32]))
+    vw("sp", p_n)
+    v_nu = []
+    for k in range(4):
+        v_nu.append(inc("sv", V.tensor_copy(T.nu[:, 256 * k:256 * k + 256], T.psa[:, 512 * k:512 * k + 256])))
+    vw("sv", v_trr)
+    sw("sv", v_trr)
+    for r in range(32):
+        dst = T.lt[:, 128 * r:128 * r + 128]
+        if r < 18:
+            v_lt = inc("sv", V.tensor_scalar(dst, T.trr[:], T.rm[:, r:r + 1], None, OP.mult))
+        else:
+            s_lt = inc("ss", S.activation(dst, T.trr[:], COPY, scale=T.rm[:, r:r + 1]))
+
+    arrive = 0
+    for q in range(N):
+        if q != rank:
+            arrive += sum(len(e) for call in sends(q, cores, topo) for d, c, e in call if c == core)
+    pw("sv", v_lt)
+    pw("ss", s_lt)
+
+    def evac(k, p):
+        sw("sp", p)
+        s = inc("ss", S.activation(T.o[:, 512 * k:512 * k + 512], T.psy[:, 512 * k:512 * k + 512], COPY))
+        SY.wait_ge(T.sem.ss, s)
+        SY.dma_start(T.y[32 * k:32 * k + 32, :], T.o[:, 512 * k:512 * k + 512]).then_inc(T.sem.dy, 16)
+
+    pend = []
+    for k in range(4):
+        h, j = k // 2, k % 2
+        win = T["tab%d" % h][:, P * j:TW]
+        v = T["v%d" % k]
+        vw("arr%d" % h, arrive)
+        sw("arr%d" % h, arrive)
+        vw("sv", v_nu[k])
+        vw("ss", done[2 * h + 1][1])
+        sw("sv", v_nu[k])
+        w = 2 if k < 3 else 1
+        for i, d in enumerate(range(0, 8, w)):
+            src = win.indirect(T.nu[:, 256 * k + 32 * d:256 * k + 32 * (d + w)])
+            dst = v[:, M * d:M * (d + w)]
+            if i % 2 == 0:
+                pw("sv", inc("sv", V.tensor_copy(dst, src)))
+            else:
+                pw("ss", inc("ss", S.activation(dst, src, COPY)))
+            for e in range(d, d + w):
+                lhs = T.lt[:, 4 * e + k::32]
+                if k < 3:
+                    p_y = inc("sp", PE.matmul(T.psy[:, 512 * k:512 * k + 512], lhs, v[:, M * e:M * e + M], e == 0, e == 7))
+                else:
+                    p_y = inc("sp", PE.matmul(T.psy[:, 1536:1792], lhs, v[:, M * e:M * e + 256], e == 0, e == 7))
+                    p_y = inc("sp", PE.matmul(T.psa[:, 0:256], lhs, v[:, M * e + 256:M * e + M], e == 0, e == 7))
+            if i == 1 and pend:
+                evac(*pend.pop())
+        pend.append((k, p_y))
+    vw("sp", p_y - 1)
+    ev = inc("sv", V.tensor_copy(T.o[:, 1536:1792], T.psy[:, 1536:1792]))
+    sw("sp", p_y)
+    es = inc("ss", S.activation(T.o[:, 1792:2048], T.psa[:, 0:256], COPY))
+    SY.wait_ge(T.sem.sv, ev)
+    SY.wait_ge(T.sem.ss, es)
+    SY.dma_start(T.y[96:128, :], T.o[:, 1536:2048]).then_inc(T.sem.dy, 16)
+    SY.wait_ge(T.sem.dy, 64)
+    g.wait_ge(T.sem.sent, sent)

@@ -1,4 +1,3 @@
-import numpy as np
 from concourse.bass import DstId, RemoteDMATransfer
 from concourse.mybir import dt, AluOpType, AxisListType, ActivationFunctionType
 
@@ -8,64 +7,120 @@ N, P, E, M, G = 8, 2048, 4096, 512, 128
 DX, DY = (-1, 0, 1, -1, 1, -1, 0, 1), (-1, -1, -1, 0, 0, 1, 1, 1)
 FAR = [[(d, s) for d in range(8) for s in range(4)
         if max(abs(2 * DX[d] + s % 2 - c % 2), abs(2 * DY[d] + s // 2 - c // 2)) > 1] for c in range(4)]
+Z = P + (N - 1) * G
 XW = E + 16
-GW = 2 * (N - 1) * G
-TW = 2 * P + GW + 16
+GW = (N - 1) * G
+BW = XW + GW
+KW = Z + 16
+KV = 1408
+MID = E // 2
 
 SCRATCH = {
-    "kl": ("sbuf", [128, 512], "int32"), "ku": ("sbuf", [128, 512], "uint16"),
-    "ni": ("sbuf", [128, 256], "int32"), "gi": ("sbuf", [128, 56], "int32"),
-    "nf": ("sbuf", [128, 256], "float32"), "gf": ("sbuf", [128, 56], "float32"),
-    "nu": ("sbuf", [128, 1024], "uint16"), "gu": ("sbuf", [128, 224], "uint16"),
-    "im": ("sbuf", [128, 128], "int32"), "im2": ("sbuf", [128, 128], "int32"),
-    "ip": ("sbuf", [128, 8], "int32"), "ip2": ("sbuf", [128, 8], "int32"), "cc": ("sbuf", [128, 8], "float32"),
-    "rm": ("sbuf", [128, 128], "float32"), "em": ("sbuf", [128, 224], "bfloat16"),
+    "kt": ("sbuf", [128, KW], "int32"),
+    "ni": ("sbuf", [128, 8, 32], "int32"), "gi": ("sbuf", [128, 56], "int32"),
+    "nu": ("sbuf", [128, 256], "uint16"), "gu": ("sbuf", [128, 56], "uint16"),
+    "og": ("sbuf", [128, GW], "float16"), "on": ("sbuf", [128, 4096], "uint16"),
+    "gl": ("sbuf", [128, 224], "uint16"), "nl": ("sbuf", [128, 1024], "uint16"),
+    "im": ("sbuf", [128, 32], "int32"), "i16": ("sbuf", [128, 32], "int32"), "i32": ("sbuf", [128, 32], "int32"),
+    "il": ("sbuf", [128, 144], "int32"), "i128": ("sbuf", [128, 144], "int32"), "sl": ("sbuf", [128, 144], "float16"),
+    "rm": ("sbuf", [128, 32], "float32"), "em": ("sbuf", [128, 176], "bfloat16"),
     "tri": ("sbuf", [128, 108], "bfloat16"), "trf": ("sbuf", [128, 128], "bfloat16"),
     "trr": ("sbuf", [128, 128], "bfloat16"), "lt": ("sbuf", [128, 4096], "bfloat16"),
     "o": ("sbuf", [128, 2048], "float32"),
     "psy": ("psum", [128, 2048], "float32"), "psa": ("psum", [128, 2048], "float32"),
 }
+for _n in range(8):
+    SCRATCH["v%d" % _n] = ("sbuf", [128, P], "bfloat16")
 for _k in range(4):
-    SCRATCH["xr%d" % _k] = ("sbuf", [128, XW], "bfloat16")
-    SCRATCH["v%d" % _k] = ("sbuf", [128, 8 * M], "bfloat16")
-for _h in range(2):
-    SCRATCH["tab%d" % _h] = ("sbuf", [128, TW], "bfloat16")
-    SCRATCH["gb%d" % _h] = ("sbuf", [128, GW], "bfloat16")
-for _n in range(6):
-    SCRATCH["na%d" % _n] = ("sbuf", [128, 256], "int32")
-for _n in range(3):
-    SCRATCH["ga%d" % _n] = ("sbuf", [128, 56], "int32")
-SEMAPHORES = (["sv", "ss", "sp", "sg", "sent", "arr0", "arr1", "dg", "dn", "dt", "dy"]
-              + ["dk%d" % k for k in range(4)] + ["dx%d" % k for k in range(4)])
+    SCRATCH["xb%d" % _k] = ("sbuf", [128, BW], "bfloat16")
+    SCRATCH["gb%d" % _k] = ("sbuf", [128, GW], "bfloat16")
+SEMAPHORES = (["sy", "sv", "ss", "sp", "sg", "sent", "dk", "dg", "dn", "dt", "dy"] + ["arr%d" % k for k in range(4)]
+              + ["hop%d" % k for k in range(1, 4)] + ["dx%d" % k for k in range(4)] + ["dm%d" % k for k in range(8)])
+UNITS = [(0, 0), (0, 1), (1, 0), (1, 1), (2, 0), (2, 1), (3, 0), (3, 1)]
 
 
 def sends(q, cores, topo):
     me = cores[q]
-    kinds = {"chip": [], "mate": [], "plane": [], "far": []}
-    for d in range(1, N):
-        c = cores[(q + d) % N]
-        a, b = topo.chip(me), topo.chip(c)
-        kinds["chip" if a == b else "mate" if topo.mates(a, b) else "plane" if topo.same_plane(a, b) else "far"].append((d, c))
-    first = kinds["far"] + kinds["mate"][:1] + kinds["plane"][:1]
-    second = kinds["mate"][1:] + kinds["plane"][1:]
+    dst = {d: cores[(q + d) % N] for d in range(1, N)}
+    home = [d for d in dst if topo.chip(dst[d]) == topo.chip(me)]
+    first = next(r for r in (range(1, 5), range(4, N)) if not set(r) & set(home))
     calls = []
-    for group in (first, second):
+    for group in (list(first), [d for d in dst if d not in first and d not in home]):
         call = []
-        for j, (d, c) in enumerate(group):
-            eng = topo.engines(me, c)
+        for j, d in enumerate(group):
+            eng = topo.engines(me, dst[d])
             n = len(eng) // len(group)
-            call.append((d, c, eng[n * j:n * j + n]))
+            call.append((d, dst[d], eng[n * j:n * j + n]))
         calls.append(call)
-    used = set(topo.engines(me, first[0][1]))
-    for d, c in kinds["chip"]:
-        calls[1].append((d, c, [e for e in topo.engines(me, c) if e not in used]))
+    used = set(topo.engines(me, dst[first[0]]))
+    for d in home:
+        calls[1].append((d, dst[d], [e for e in topo.engines(me, dst[d]) if e not in used][::2]))
     return calls
+
+
+def shared(eng, n):
+    return [eng[len(eng) // n * j:len(eng) // n * (j + 1)] for j in range(n)]
+
+
+def relays(q, cores, topo):
+    me = cores[q]
+    dst = {d: cores[(q + d) % N] for d in range(1, N)}
+    kinds = {"home": [], "mate": [], "plane": [], "far": []}
+    for d in dst:
+        a, b = topo.chip(me), topo.chip(dst[d])
+        kinds["home" if a == b else "mate" if topo.mates(a, b) else "plane" if topo.same_plane(a, b) else "far"].append(d)
+    off = topo.engines(me, dst[kinds["far"][0]])
+    inner = [e for e in topo.engines(me, dst[kinds["home"][0]]) if e not in off]
+    own = [(d, dst[d], e) for d, e in zip(kinds["far"], shared(off, 2))] + [(d, dst[d], inner) for d in kinds["home"]]
+    free = [c for c in topo.cores_of(me) if c not in cores and topo.die(c) == topo.die(me)]
+    hands = []
+    for kind, eng in zip(("mate", "plane"), shared(inner, 2)):
+        h = next(c for c in free if topo.may_write(c, dst[kinds[kind][0]]))
+        free.remove(h)
+        hands.append((h, eng, [(d, dst[d], e) for d, e in zip(kinds[kind], shared(topo.engines(h, dst[kinds[kind][0]]), 2))]))
+    return own, hands
+
+
+def transfer(T, topo, core, eng, sem, src, dst):
+    ad = topo.addr(core)
+    return RemoteDMATransfer(dst_ids=[DstId(rid=ad[0], pnc=ad[1])], dma_engine_mask=sum(1 << e for e in eng),
+                             remote_sem=T.sem[sem], src=src, dst=dst)
+
+
+def to_ranks(g, T, topo, k, call):
+    g.remote_dma_fused([transfer(T, topo, c, eng, "arr%d" % k, T["gb%d" % k][:, G * (d - 1):G * d],
+                                 T["xb%d" % k][:, XW + G * (d - 1):XW + G * d]) for d, c, eng in call], local_sem=T.sem.sent)
+    return sum(len(eng) for d, c, eng in call)
+
+
+def helper_program(g, core, T, topo):
+    cores = list(T.cores)
+    for q in range(N):
+        for h, eng, call in relays(q, cores, topo)[1]:
+            if h == core:
+                sent = 0
+                for k in (1, 2, 3):
+                    g.wait_ge(T.sem["hop%d" % k], len(eng))
+                    sent += to_ranks(g, T, topo, k, call)
+                g.wait_ge(T.sem.sent, sent)
+
+
+def runs():
+    pos = [32 * c + 4 * d + s for c in range(4) for d, s in FAR[c]]
+    out, i = [], 0
+    while i < len(pos):
+        j = i
+        while j + 1 < len(pos) and pos[j + 1] == pos[j] + 1:
+            j += 1
+        out.append((pos[i], i, j + 1 - i))
+        i = j + 1
+    return out
 
 
 def rank_program(g, core, T, topo):
     rank = T.rank_of(core)
     if rank is None:
-        return
+        return helper_program(g, core, T, topo)
     cores = list(T.cores)
     V, S, PE, SY = g.vector, g.scalar, g.tensor, g.sync
     cnt = {"sv": 0, "ss": 0, "sp": 0, "sg": 0}
@@ -90,214 +145,221 @@ def rank_program(g, core, T, topo):
     def pw(name, n):
         wait("P", PE, name, n)
 
-    def load_k(q, k):
+    def yw(name, n):
+        wait("Y", SY, name, n)
+
+    def load_x(q, k, w):
         for s in range(4):
-            q.dma_start(T.kl[32 * s:32 * s + 32, 128 * k:128 * k + 128],
-                        T.kid[2 * k:2 * k + 2, P * s:P * s + P]).then_inc(T.sem["dk%d" % k], 16)
+            q.dma_start(T["xb%d" % k][64 * w + 16 * s:64 * w + 16 * s + 16, 0:E],
+                        T.ex[32 * k + 16 * w:32 * k + 16 * w + 16, :]).then_inc(T.sem["dx%d" % k], 16)
 
-    def load_x(q, k, ss):
-        for s in ss:
-            q.dma_start(T["xr%d" % k][32 * s:32 * s + 32, 0:E], T.ex[32 * k:32 * k + 32, :]).then_inc(T.sem["dx%d" % k], 16)
+    def iota(out, pattern, base, mult):
+        wait("G", g, "sg", cnt["sg"])
+        return inc("sg", g.iota(out, pattern, base, mult))
 
-    S.dma_start(T.gi[:], T.give[:]).then_inc(T.sem.dg, 16)
-    S.dma_start(T.ni[:], T.near[:]).then_inc(T.sem.dn, 16)
-    load_k(SY, 0)
-    load_x(SY, 0, (0, 1))
-    load_x(S, 0, (2, 3))
-    S.dma_start(T.tri[:], T.tr[:]).then_inc(T.sem.dt, 16)
-    load_k(SY, 1)
-    load_x(SY, 1, (0, 1))
-    load_x(S, 1, (2, 3))
-    for k in (2, 3):
-        load_k(SY, k)
-        load_x(SY, k, (0, 1, 2, 3))
-
-    i1 = inc("sg", g.iota(T.im[:], [[-1, 128]], 128, 1))
-    i2 = inc("sg", g.iota(T.ip[:], [[0, 8]], 0, 1))
+    m_k = inc("sv", V.memset(T.kt[:, 0:KV], MID))
+    g_k = iota(T.kt[:, KV:P], [[0, P - KV]], MID, 0)
     m_trf = inc("sv", V.memset(T.trf[:], 0.0))
+    inc("sv", V.memset(T.em[:], 0.0))
+    inc("sv", V.memset(T.rm[:], 0.0))
     for k in range(4):
-        m_x = inc("sv", V.memset(T["xr%d" % k][:, E:XW], 0.0))
-    for h in range(2):
-        m_t = inc("sv", V.memset(T["tab%d" % h][:, 2 * P + GW:TW], 0.0))
-    m_em = inc("sv", V.memset(T.em[:], 0.0))
-    vw("sg", i2)
-    a = inc("sv", V.tensor_scalar(T.im2[:], T.im[:], 31, None, OP.bitwise_and))
-    b = inc("sv", V.tensor_scalar(T.ip2[:], T.ip[:], 5, 1, OP.arith_shift_right, OP.bitwise_and))
+        inc("sv", V.memset(T["xb%d" % k][:, E:XW], 0.0))
+    m_z = inc("sv", V.memset(T.kt[:, Z:KW], E))
+    g_im = iota(T.im[:], [[-1, 32]], 128, 1)
+    g_il = iota(T.il[:], [[-1, 144]], 143, 4)
+    g_kt = iota(T.kt[:, P:Z], [[1, GW]], XW, 0)
+    vw("sg", g_im)
+    inc("sv", V.tensor_scalar(T.i32[:], T.im[:], 31, None, OP.bitwise_and))
+    a = inc("sv", V.tensor_scalar(T.i16[:], T.im[:], 15, None, OP.bitwise_and))
+    vw("sg", g_il)
+    b = inc("sv", V.tensor_scalar(T.i128[:], T.il[:], 127, None, OP.bitwise_and))
     vw("sv", a)
-    v_rm = inc("sv", V.tensor_scalar(T.rm[:], T.im2[:], 0, None, OP.is_equal))
+    for w in range(2):
+        v_em = inc("sv", V.tensor_scalar(T.em[:, 48 + 64 * w:64 + 64 * w], T.i32[:, 16 * w:16 * w + 16], 0, None, OP.is_equal))
+    for w in range(2):
+        v_rm = inc("sv", V.tensor_scalar(T.rm[64 * w:64 * w + 64, 16 * w:16 * w + 16], T.i16[64 * w:64 * w + 64, 0:16],
+                                         0, None, OP.is_equal))
     vw("sv", b)
-    v_cc = inc("sv", V.tensor_scalar(T.cc[:], T.ip2[:], -2047, 2047, OP.mult, OP.add))
-    vw("sv", v_rm)
-    v_em = inc("sv", V.tensor_copy(T.em[:, 96:128], T.rm[:, 0:32]))
+    inc("sv", V.tensor_scalar(T.sl[:], T.i128[:], 0, None, OP.is_equal))
 
+    SY.dma_start(T.gi[:], T.give[:]).then_inc(T.sem.dg, 16)
+    S.dma_start(T.tri[:], T.tr[:]).then_inc(T.sem.dt, 16)
+    S.dma_start(T.ni[:], T.near[:]).then_inc(T.sem.dn, 16)
+    load_x(SY, 0, 0)
+    yw("sv", m_k)
+    yw("sg", g_k)
+    SY.dma_start(T.kt[0:128:4, 0:P], T.kid[:]).then_inc(T.sem.dk, 16)
+    load_x(SY, 0, 1)
+    sw("sv", m_k)
+    load_x(S, 1, 0)
+    load_x(SY, 1, 1)
+    for w in range(2):
+        load_x(SY, 2, w)
+
+    rs = runs()
     sw("dt", 16)
     sw("sv", m_trf)
-    for c in range(4):
-        pos = [4 * d + s for d, s in FAR[c]]
-        i = 0
-        while i < 27:
-            j = i
-            while j + 1 < 27 and pos[j + 1] == pos[j] + 1:
-                j += 1
-            s_trf = inc("ss", S.activation(T.trf[:, 32 * c + pos[i]:32 * c + pos[j] + 1],
-                                           T.tri[:, 27 * c + i:27 * c + j + 1], COPY))
-            i = j + 1
-
+    for pos, i, n in rs[:11]:
+        s_trf = inc("ss", S.activation(T.trf[:, pos:pos + n], T.tri[:, i:i + n], COPY))
     vw("dg", 16)
-    g1 = inc("sv", V.tensor_scalar(T.ga0[:], T.gi[:], 16, None, OP.mult))
-    g2 = inc("sv", V.tensor_scalar(T.ga1[:], T.gi[:], 7, None, OP.arith_shift_right))
+    v_gu = inc("sv", V.tensor_copy(T.gu[:], T.gi[:]))
+    vw("dt", 16)
+    for pos, i, n in rs[11:]:
+        v_trf = inc("sv", V.tensor_copy(T.trf[:, pos:pos + n], T.tri[:, i:i + n]))
     vw("dn", 16)
-    n1 = inc("sv", V.tensor_scalar(T.na0[:], T.ni[:], P - 1, 16, OP.min, OP.mult))
-    vw("sv", g2)
-    g3 = inc("sv", V.tensor_scalar(T.ga2[:], T.ga1[:], -2047, None, OP.mult))
-    n3 = inc("sv", V.tensor_scalar(T.na2[:], T.ni[:], P - 1, 2, OP.max, OP.mult))
-    vw("sv", g3)
-    g4 = inc("sv", V.tensor_tensor(T.gf[:], T.ga0[:], T.ga2[:], OP.add))
-    n2 = inc("sv", V.tensor_scalar(T.na1[:], T.na0[:], 11, None, OP.arith_shift_right))
-    n4 = inc("sv", V.tensor_scalar(T.na3[:], T.ni[:], P, T.cc[:, 0:1], OP.is_ge, OP.mult))
-    vw("sv", n2)
-    n5 = inc("sv", V.tensor_scalar(T.na4[:], T.na1[:], -2047, -4094, OP.mult, OP.add))
-    vw("dk0", 64)
-    v_ku = [inc("sv", V.tensor_copy(T.ku[:, 0:128], T.kl[:, 0:128]))]
-    pw("sv", g4)
-    for k in range(4):
-        p_g = inc("sp", PE.matmul(T.psy[:, 512 * k:512 * k + 56], T.rm[32 * k:32 * k + 32, :], T.gf[32 * k:32 * k + 32, :], True, True))
-    vw("sp", p_g)
-    for k in range(4):
-        v_gu = inc("sv", V.tensor_copy(T.gu[:, 56 * k:56 * k + 56], T.psy[:, 512 * k:512 * k + 56]))
-    vw("sv", n4)
-    n6 = inc("sv", V.tensor_tensor(T.na5[:], T.na0[:], T.na2[:], OP.add))
-    vw("sv", n5)
-    n7 = inc("sv", V.tensor_tensor(T.na1[:], T.na3[:], T.na4[:], OP.add))
-    vw("sv", n7)
-    n8 = inc("sv", V.tensor_tensor(T.nf[:], T.na5[:], T.na1[:], OP.add))
+    for x in range(2):
+        v_nu = inc("sv", V.tensor_copy(T.nu[:, 128 * x:128 * x + 128], T.ni[:, :, 16 * x:16 * x + 16]))
+
     pw("ss", s_trf)
-    pw("sv", max(v_em, v_gu))
+    pw("sv", v_trf)
     for k in range(4):
         for s in range(4):
-            op = PE.matmul(T.psy[:, 512 * k:512 * k + 32], T.em[32 * k:32 * k + 32, 96 - 32 * s:224 - 32 * s],
-                           T.trf[32 * k:32 * k + 32, s::4], s == 0, s == 3)
-            p_t = inc("sp", op)
-    pw("sv", n8)
+            p_t = inc("sp", PE.matmul(T.psy[:, 512 * k:512 * k + 32], T.em[32 * k:32 * k + 32, 48 - 16 * s:176 - 16 * s],
+                                      T.trf[32 * k:32 * k + 32, s::4], s == 0, s == 3))
+    sw("sp", p_t)
     for k in range(4):
-        p_n = inc("sp", PE.matmul(T.psa[:, 512 * k:512 * k + 256], T.rm[32 * k:32 * k + 32, :], T.nf[32 * k:32 * k + 32, :], True, True))
+        s_trr = inc("ss", S.activation(T.trr[:, k::4], T.psy[:, 512 * k:512 * k + 32], COPY))
+    last_lt = {}
 
-    VC, GC = 64, 28
-    done = {}
+    def stationary(on_vector, rows):
+        for r in rows:
+            dst = T.lt[:, 128 * r:128 * r + 128]
+            if on_vector:
+                vw("ss", s_trr)
+                last_lt["sv"] = inc("sv", V.tensor_scalar(dst, T.trr[:], T.rm[:, r:r + 1], None, OP.mult))
+            else:
+                sw("ss", s_trr)
+                sw("sv", v_rm)
+                last_lt["ss"] = inc("ss", S.activation(dst, T.trr[:], COPY, scale=T.rm[:, r:r + 1]))
 
-    def level1(k):
-        h, j = k // 2, k % 2
-        x, t = T["xr%d" % k], T["tab%d" % h]
-        vw("dx%d" % k, 64)
-        vw("sv", max(v_ku[k], m_x))
-        lv = inc("sv", V.tensor_copy(t[:, P * j:P * j + 16 * VC], x[:, 0:XW].indirect(T.ku[:, 128 * k:128 * k + VC])))
-        sw("dx%d" % k, 64)
-        sw("sv", max(v_ku[k], m_x))
-        ls = inc("ss", S.activation(t[:, P * j + 16 * VC:P * j + P], x[:, 0:XW].indirect(T.ku[:, 128 * k + VC:128 * k + 128]), COPY))
-        done[k] = (lv, ls)
+    stationary(False, range(0, 10))
 
-    def conv(k):
-        vw("dk%d" % k, 64)
-        v_ku.append(inc("sv", V.tensor_copy(T.ku[:, 128 * k:128 * k + 128], T.kl[:, 128 * k:128 * k + 128])))
-
-    def ghosts(k):
-        h, j = k // 2, k % 2
-        t, b = T["tab%d" % h], T["gb%d" % h]
-        lv, ls = done[k]
-        w = t[:, P * j:P * j + P]
-        vw("sv", max(lv, v_gu))
-        vw("ss", ls)
-        gv = inc("sv", V.tensor_copy(b[:, j:32 * GC:2], w.indirect(T.gu[:, 56 * k:56 * k + GC])))
-        sw("ss", ls)
-        sw("sv", max(lv, v_gu))
-        gs = inc("ss", S.activation(b[:, 32 * GC + j:GW:2], w.indirect(T.gu[:, 56 * k + GC:56 * k + 56]), COPY))
-        return gv, gs
-
-    plan = sends(rank, cores, topo)
-    sent = 0
-    for h in range(2):
-        for k in (2 * h, 2 * h + 1):
-            if k:
-                conv(k)
-            level1(k)
-            gv, gs = ghosts(k)
-        g.wait_ge(T.sem.sv, gv)
-        g.wait_ge(T.sem.ss, gs)
-        b, t = T["gb%d" % h], T["tab%d" % h]
-        for call in plan:
-            tr = []
-            for d, c, eng in call:
-                ad = topo.addr(c)
-                lo = 2 * G * (d - 1)
-                tr.append(RemoteDMATransfer(dst_ids=[DstId(rid=ad[0], pnc=ad[1])], dma_engine_mask=sum(1 << e for e in eng),
-                                            remote_sem=T.sem["arr%d" % h], src=b[:, lo:lo + 2 * G],
-                                            dst=t[:, 2 * P + lo:2 * P + lo + 2 * G]))
-                sent += len(eng)
-            g.remote_dma_fused(tr, local_sem=T.sem.sent)
-
-    vw("sp", p_t)
+    vw("dk", 16)
+    vw("sv", v_nu)
+    pw("sv", inc("sv", V.tensor_scalar(T.og[:], T.kt[:, 0:P].indirect(T.gu[:]), -MID, None, OP.add)))
+    p_g = []
     for k in range(4):
-        v_trr = inc("sv", V.tensor_copy(T.trr[:, k::4], T.psy[:, 512 * k:512 * k + 32]))
-    vw("sp", p_n)
-    v_nu = []
-    for k in range(4):
-        v_nu.append(inc("sv", V.tensor_copy(T.nu[:, 256 * k:256 * k + 256], T.psa[:, 512 * k:512 * k + 256])))
-    vw("sv", v_trr)
-    sw("sv", v_trr)
-    for r in range(32):
-        dst = T.lt[:, 128 * r:128 * r + 128]
-        if r < 18:
-            v_lt = inc("sv", V.tensor_scalar(dst, T.trr[:], T.rm[:, r:r + 1], None, OP.mult))
-        else:
-            s_lt = inc("ss", S.activation(dst, T.trr[:], COPY, scale=T.rm[:, r:r + 1]))
+        for a in range(16):
+            p = inc("sp", PE.matmul(T.psa[:, 512 * k:512 * k + 56], T.sl[32 * k:32 * k + 32, 15 - a:143 - a],
+                                    T.og[32 * k:32 * k + 32, a::16], a == 0, a == 15))
+        p_g.append(p)
+    v_gl = {}
 
-    arrive = 0
+    def give_list(k):
+        vw("sp", p_g[k])
+        v_gl[k] = inc("sv", V.tensor_scalar(T.gl[:, 56 * k:56 * k + 56], T.psa[:, 512 * k:512 * k + 56], MID, None, OP.add))
+
+    def numbers(lo, hi):
+        vw("sg", g_kt)
+        return inc("sv", V.tensor_copy(T.on[:, 16 * lo:16 * hi], T.kt[:, 0:KW].indirect(T.nu[:, lo:hi])))
+
+    def near_lists(x, done):
+        yw("sv", done)
+        for k in range(4):
+            SY.dma_start(T.nl[:, 256 * k + 128 * x:256 * k + 128 * x + 128],
+                         T.on[32 * k:32 * k + 32:4, P * x:P * x + P]).then_inc(T.sem["dm%d" % (2 * k + x)], 16)
+        SY.sem_inc(T.sem.sy, 1)
+
+    def ghosts(on_vector, k, lo, hi):
+        src = T["xb%d" % k][:, 0:XW].indirect(T.gl[:, 56 * k + lo:56 * k + hi])
+        dst = T["gb%d" % k][:, 16 * lo:16 * hi]
+        w = vw if on_vector else sw
+        w("dx%d" % k, 128)
+        w("sv", v_gl[k])
+        return ("sv", inc("sv", V.tensor_copy(dst, src))) if on_vector else ("ss", inc("ss", S.activation(dst, src, COPY)))
+
+    own, hands = relays(rank, cores, topo)
+    sent = [0]
+
+    def send(k, call, ready):
+        for name, n in ready:
+            wait("G", g, name, n)
+        sent[0] += to_ranks(g, T, topo, k, call)
+
+    def hand_on(k, ready):
+        for name, n in ready:
+            wait("G", g, name, n)
+        tr = []
+        for h, eng, call in hands:
+            lo = G * (min(d for d, c, e in call) - 1)
+            tr.append(transfer(T, topo, h, eng, "hop%d" % k, T["gb%d" % k][:, lo:lo + 2 * G], T["gb%d" % k][:, lo:lo + 2 * G]))
+            sent[0] += len(eng)
+        g.remote_dma_fused(tr, local_sem=T.sem.sent)
+
+    numbers(0, 24)
+    give_list(0)
+    for call in sends(rank, cores, topo):
+        lo, hi = 8 * min(d - 1 for d, c, e in call), 8 * max(d for d, c, e in call)
+        mid = (lo + hi) // 2
+        send(0, call, [ghosts(True, 0, lo, mid), ghosts(False, 0, mid, hi)])
+    for k in (1, 2, 3):
+        give_list(k)
+    near_lists(0, numbers(24, 128))
+    load_x(SY, 3, 0)
+    near_lists(1, numbers(128, 256))
+    load_x(SY, 3, 1)
+    for k, rows in ((1, range(10, 16)), (2, range(16, 28))):
+        hand_on(k, [ghosts(False, k, 0, 56)])
+        send(k, own, [("sy", k)])
+        stationary(False, rows)
+    stationary(True, range(28, 32))
+
+    arrive = [0, 0]
     for q in range(N):
-        if q != rank:
-            arrive += sum(len(e) for call in sends(q, cores, topo) for d, c, e in call if c == core)
-    pw("sv", v_lt)
-    pw("ss", s_lt)
+        theirs, their_hands = relays(q, cores, topo)
+        arrive[0] += sum(len(e) for call in sends(q, cores, topo) for d, c, e in call if c == core)
+        arrive[1] += sum(len(e) for call in [theirs] + [x[2] for x in their_hands] for d, c, e in call if c == core)
+    pw("sv", last_lt["sv"])
+    pw("ss", last_lt["ss"])
+    copied = {}
 
-    def evac(k, p):
+    def bank(n):
+        return (T.psa, 512 * n) if n < 4 else (T.psy, 512 * (n - 4))
+
+    def evac(on_vector, ps, col, n, dst, p):
+        if on_vector:
+            vw("sp", p)
+            return "sv", inc("sv", V.tensor_copy(T.o[:, dst:dst + n], ps[:, col:col + n]))
         sw("sp", p)
-        s = inc("ss", S.activation(T.o[:, 512 * k:512 * k + 512], T.psy[:, 512 * k:512 * k + 512], COPY))
-        SY.wait_ge(T.sem.ss, s)
+        return "ss", inc("ss", S.activation(T.o[:, dst:dst + n], ps[:, col:col + n], COPY))
+
+    def store(k):
+        for name, n in copied[k]:
+            yw(name, n)
         SY.dma_start(T.y[32 * k:32 * k + 32, :], T.o[:, 512 * k:512 * k + 512]).then_inc(T.sem.dy, 16)
 
     pend = []
-    for k in range(4):
-        h, j = k // 2, k % 2
-        win = T["tab%d" % h][:, P * j:TW]
-        v = T["v%d" % k]
-        vw("arr%d" % h, arrive)
-        sw("arr%d" % h, arrive)
-        vw("sv", v_nu[k])
-        vw("ss", done[2 * h + 1][1])
-        sw("sv", v_nu[k])
-        w = 2 if k < 3 else 1
-        for i, d in enumerate(range(0, 8, w)):
-            src = win.indirect(T.nu[:, 256 * k + 32 * d:256 * k + 32 * (d + w)])
-            dst = v[:, M * d:M * (d + w)]
-            if i % 2 == 0:
-                pw("sv", inc("sv", V.tensor_copy(dst, src)))
-            else:
-                pw("ss", inc("ss", S.activation(dst, src, COPY)))
-            for e in range(d, d + w):
-                lhs = T.lt[:, 4 * e + k::32]
-                if k < 3:
-                    p_y = inc("sp", PE.matmul(T.psy[:, 512 * k:512 * k + 512], lhs, v[:, M * e:M * e + M], e == 0, e == 7))
-                else:
-                    p_y = inc("sp", PE.matmul(T.psy[:, 1536:1792], lhs, v[:, M * e:M * e + 256], e == 0, e == 7))
-                    p_y = inc("sp", PE.matmul(T.psa[:, 0:256], lhs, v[:, M * e + 256:M * e + M], e == 0, e == 7))
-            if i == 1 and pend:
-                evac(*pend.pop())
-        pend.append((k, p_y))
-    vw("sp", p_y - 1)
-    ev = inc("sv", V.tensor_copy(T.o[:, 1536:1792], T.psy[:, 1536:1792]))
-    sw("sp", p_y)
-    es = inc("ss", S.activation(T.o[:, 1792:2048], T.psa[:, 0:256], COPY))
-    SY.wait_ge(T.sem.sv, ev)
-    SY.wait_ge(T.sem.ss, es)
-    SY.dma_start(T.y[96:128, :], T.o[:, 1536:2048]).then_inc(T.sem.dy, 16)
+    for n, (k, x) in enumerate(UNITS):
+        win = T["xb%d" % k][:, 0:BW]
+        v = T["v%d" % n]
+        ps, col = bank(n)
+        base = 256 * k + 128 * x
+        if n == 2:
+            hand_on(3, [ghosts(True, 3, 0, 28), ghosts(False, 3, 28, 56)])
+            send(3, own, [])
+        for w in (vw, sw):
+            w("arr%d" % k, arrive[min(k, 1)])
+            w("dm%d" % (2 * k + x), 16)
+            w("dx%d" % k, 128)
+        last = n == len(UNITS) - 1
+        for lo, hi in ([(0, 64), (64, 128)] if last else [(0, 128)]):
+            mid = (lo + hi) // 2
+            pw("sv", inc("sv", V.tensor_copy(v[:, 16 * lo:16 * mid], win.indirect(T.nl[:, base + lo:base + mid]))))
+            pw("ss", inc("ss", S.activation(v[:, 16 * mid:16 * hi], win.indirect(T.nl[:, base + mid:base + hi]), COPY)))
+            p_e = []
+            for e in range(2):
+                out = T.psa[:, lo:hi] if last and e else ps[:, col + 128 * e + lo:col + 128 * e + hi]
+                for d in range(8):
+                    p_y = inc("sp", PE.matmul(out, T.lt[:, 4 * d + k::32], v[:, 16 * lo + 2 * d + e:16 * hi:16], d == 0, d == 7))
+                p_e.append(p_y)
+            if len(pend) == 2 or last:
+                pn, pk, px, pp = pend.pop(0)
+                copied.setdefault(pk, []).append(evac(pn % 2 == 1, bank(pn)[0], bank(pn)[1], 256, 512 * pk + 256 * px, pp))
+                if px:
+                    store(pk)
+        pend.append((n, k, x, p_y))
+    copied[k].append(evac(True, ps, col, 128, 512 * k + 256 * x, p_e[0]))
+    copied[k].append(evac(False, T.psa, 0, 128, 512 * k + 256 * x + 128, p_e[1]))
+    store(k)
     SY.wait_ge(T.sem.dy, 64)
-    g.wait_ge(T.sem.sent, sent)
+    g.wait_ge(T.sem.sent, sent[0])

@@ -13,6 +13,9 @@ GW = (N - 1) * G
 BW = XW + GW
 KW = Z + 16
 KV = 1408
+PARTS = (144, 112)
+LS = 26
+GV = 24
 MID = E // 2
 
 SCRATCH = {
@@ -29,14 +32,16 @@ SCRATCH = {
     "o": ("sbuf", [128, 2048], "float32"),
     "psy": ("psum", [128, 2048], "float32"), "psa": ("psum", [128, 2048], "float32"),
 }
-for _n in range(8):
-    SCRATCH["v%d" % _n] = ("sbuf", [128, P], "bfloat16")
+for _n in range(9):
+    SCRATCH["v%d" % _n] = ("sbuf", [128, 16 * max(PARTS)], "bfloat16")
 for _k in range(4):
     SCRATCH["xb%d" % _k] = ("sbuf", [128, BW], "bfloat16")
     SCRATCH["gb%d" % _k] = ("sbuf", [128, GW], "bfloat16")
-SEMAPHORES = (["sy", "sv", "ss", "sp", "sg", "sent", "dk", "dg", "dn", "dt", "dy"] + ["arr%d" % k for k in range(4)]
+SEMAPHORES = (["sy", "dl", "sv", "ss", "sp", "sg", "sent", "dk", "dg", "dn", "dt", "dy"] + ["arr%d" % k for k in range(4)]
               + ["hop%d" % k for k in range(1, 4)] + ["dx%d" % k for k in range(4)] + ["dm%d" % k for k in range(8)])
-UNITS = [(0, 0), (0, 1), (1, 0), (1, 1), (2, 0), (2, 1), (3, 0), (3, 1)]
+UNITS = [(0, 0, 0, 58, 144, "V"), (0, 1, 0, 52, 112, "V"), (1, 0, 0, 66, 144, "V"), (1, 1, 0, 52, 112, "V"),
+         (2, 0, 0, 66, 144, "V"), (2, 1, 0, 52, 112, "V"), (3, 1, 0, 52, 112, "V"),
+         (3, 0, 0, 36, 80, "VV"), (3, 0, 80, 110, 144, "VV")]
 
 
 def sends(q, cores, topo):
@@ -153,33 +158,29 @@ def rank_program(g, core, T, topo):
             q.dma_start(T["xb%d" % k][64 * w + 16 * s:64 * w + 16 * s + 16, 0:E],
                         T.ex[32 * k + 16 * w:32 * k + 16 * w + 16, :]).then_inc(T.sem["dx%d" % k], 16)
 
-    def iota(out, pattern, base, mult):
+    def iota(out, pattern, base, mult, **kw):
         wait("G", g, "sg", cnt["sg"])
-        return inc("sg", g.iota(out, pattern, base, mult))
+        return inc("sg", g.iota(out, pattern, base, mult, **kw))
 
+    m_lt = inc("sv", V.memset(T.lt[:, 0:512], 0.0))
     m_k = inc("sv", V.memset(T.kt[:, 0:KV], MID))
     g_k = iota(T.kt[:, KV:P], [[0, P - KV]], MID, 0)
-    m_trf = inc("sv", V.memset(T.trf[:], 0.0))
+    inc("sv", V.memset(T.lt[:, 3072:4096], 0.0))
     inc("sv", V.memset(T.em[:], 0.0))
-    inc("sv", V.memset(T.rm[:], 0.0))
-    for k in range(4):
-        inc("sv", V.memset(T["xb%d" % k][:, E:XW], 0.0))
-    m_z = inc("sv", V.memset(T.kt[:, Z:KW], E))
+    inc("sv", V.memset(T.trf[:], 0.0))
     g_im = iota(T.im[:], [[-1, 32]], 128, 1)
     g_il = iota(T.il[:], [[-1, 144]], 143, 4)
-    g_kt = iota(T.kt[:, P:Z], [[1, GW]], XW, 0)
+    iota(T.kt[:, P:Z], [[1, GW]], XW, 0)
+    g_kt = iota(T.kt[:, Z:KW], [[0, KW - Z]], E, 0)
     vw("sg", g_im)
-    inc("sv", V.tensor_scalar(T.i32[:], T.im[:], 31, None, OP.bitwise_and))
-    a = inc("sv", V.tensor_scalar(T.i16[:], T.im[:], 15, None, OP.bitwise_and))
-    vw("sg", g_il)
-    b = inc("sv", V.tensor_scalar(T.i128[:], T.il[:], 127, None, OP.bitwise_and))
+    a = inc("sv", V.tensor_scalar(T.i32[:], T.im[:], 31, None, OP.bitwise_and))
+    vw("dg", 16)
+    v_gu = inc("sv", V.tensor_copy(T.gu[:], T.gi[:]))
     vw("sv", a)
     for w in range(2):
         v_em = inc("sv", V.tensor_scalar(T.em[:, 48 + 64 * w:64 + 64 * w], T.i32[:, 16 * w:16 * w + 16], 0, None, OP.is_equal))
-    for w in range(2):
-        v_rm = inc("sv", V.tensor_scalar(T.rm[64 * w:64 * w + 64, 16 * w:16 * w + 16], T.i16[64 * w:64 * w + 64, 0:16],
-                                         0, None, OP.is_equal))
-    vw("sv", b)
+    vw("sg", g_il)
+    vw("sv", inc("sv", V.tensor_scalar(T.i128[:], T.il[:], 127, None, OP.bitwise_and)))
     inc("sv", V.tensor_scalar(T.sl[:], T.i128[:], 0, None, OP.is_equal))
 
     SY.dma_start(T.gi[:], T.give[:]).then_inc(T.sem.dg, 16)
@@ -190,74 +191,67 @@ def rank_program(g, core, T, topo):
     yw("sg", g_k)
     SY.dma_start(T.kt[0:128:4, 0:P], T.kid[:]).then_inc(T.sem.dk, 16)
     load_x(SY, 0, 1)
-    sw("sv", m_k)
-    load_x(S, 1, 0)
-    load_x(SY, 1, 1)
-    for w in range(2):
-        load_x(SY, 2, w)
+    for k, w in ((1, 0), (1, 1), (2, 0), (2, 1), (3, 0)):
+        load_x(SY, k, w)
 
-    rs = runs()
-    sw("dt", 16)
-    sw("sv", m_trf)
-    for pos, i, n in rs[:11]:
-        s_trf = inc("ss", S.activation(T.trf[:, pos:pos + n], T.tri[:, i:i + n], COPY))
-    vw("dg", 16)
-    v_gu = inc("sv", V.tensor_copy(T.gu[:], T.gi[:]))
+    sw("sv", m_lt)
+    sw("ss", inc("ss", S.activation(T.lt[:, 512:1024], T.lt[:, 0:512], COPY)))
+    inc("ss", S.activation(T.lt[:, 1024:2048], T.lt[:, 0:1024], COPY))
+    for k in range(4):
+        s_z = inc("ss", S.activation(T["xb%d" % k][:, E:XW], T.lt[:, 0:XW - E], COPY))
+    s_lt = inc("ss", S.activation(T.lt[:, 2048:3072], T.lt[:, 0:1024], COPY))
     vw("dt", 16)
-    for pos, i, n in rs[11:]:
+    for pos, i, n in runs():
         v_trf = inc("sv", V.tensor_copy(T.trf[:, pos:pos + n], T.tri[:, i:i + n]))
-    vw("dn", 16)
-    for x in range(2):
-        v_nu = inc("sv", V.tensor_copy(T.nu[:, 128 * x:128 * x + 128], T.ni[:, :, 16 * x:16 * x + 16]))
-
-    pw("ss", s_trf)
     pw("sv", v_trf)
     for k in range(4):
         for s in range(4):
             p_t = inc("sp", PE.matmul(T.psy[:, 512 * k:512 * k + 32], T.em[32 * k:32 * k + 32, 48 - 16 * s:176 - 16 * s],
                                       T.trf[32 * k:32 * k + 32, s::4], s == 0, s == 3))
-    sw("sp", p_t)
-    for k in range(4):
-        s_trr = inc("ss", S.activation(T.trr[:, k::4], T.psy[:, 512 * k:512 * k + 32], COPY))
-    last_lt = {}
-
-    def stationary(on_vector, rows):
-        for r in rows:
-            dst = T.lt[:, 128 * r:128 * r + 128]
-            if on_vector:
-                vw("ss", s_trr)
-                last_lt["sv"] = inc("sv", V.tensor_scalar(dst, T.trr[:], T.rm[:, r:r + 1], None, OP.mult))
-            else:
-                sw("ss", s_trr)
-                sw("sv", v_rm)
-                last_lt["ss"] = inc("ss", S.activation(dst, T.trr[:], COPY, scale=T.rm[:, r:r + 1]))
-
-    stationary(False, range(0, 10))
+    cut = PARTS[0]
 
     vw("dk", 16)
-    vw("sv", v_nu)
-    pw("sv", inc("sv", V.tensor_scalar(T.og[:], T.kt[:, 0:P].indirect(T.gu[:]), -MID, None, OP.add)))
-    p_g = []
-    for k in range(4):
-        for a in range(16):
-            p = inc("sp", PE.matmul(T.psa[:, 512 * k:512 * k + 56], T.sl[32 * k:32 * k + 32, 15 - a:143 - a],
-                                    T.og[32 * k:32 * k + 32, a::16], a == 0, a == 15))
-        p_g.append(p)
-    v_gl = {}
+    vw("sv", v_gu)
+    first = sends(rank, cores, topo)
+    spans = [(8 * min(d - 1 for d, c, e in call), 8 * max(d for d, c, e in call)) for call in first]
+    v_og = [inc("sv", V.tensor_scalar(T.og[:, 16 * lo:16 * hi], T.kt[:, 0:P].indirect(T.gu[:, lo:hi]), -MID, None, OP.add))
+            for lo, hi in spans]
+    vw("dn", 16)
+    inc("sv", V.tensor_copy(T.nu[:, 0:cut], T.ni[:, :, 0:cut // 8]))
+    v_nu = inc("sv", V.tensor_copy(T.nu[:, cut:256], T.ni[:, :, cut // 8:32]))
 
-    def give_list(k):
-        vw("sp", p_g[k])
-        v_gl[k] = inc("sv", V.tensor_scalar(T.gl[:, 56 * k:56 * k + 56], T.psa[:, 512 * k:512 * k + 56], MID, None, OP.add))
+    jobs = [(0, 0) + spans[0], (0, 3) + spans[1], (1, 1, 0, 56), (2, 2, 0, 56), (3, 0, 0, 56)]
+    p_g, v_gl = {}, {}
+
+    def turn(j):
+        k, b, lo, hi = jobs[j]
+        for a in range(16):
+            p_g[j] = inc("sp", PE.matmul(T.psa[:, 512 * b:512 * b + hi - lo], T.sl[32 * k:32 * k + 32, 15 - a:143 - a],
+                                         T.og[32 * k:32 * k + 32, 16 * lo + a:16 * hi:16], a == 0, a == 15))
+
+    def give_list(j):
+        k, b, lo, hi = jobs[j]
+        vw("sp", p_g[j])
+        v_gl[k] = inc("sv", V.tensor_scalar(T.gl[:, 56 * k + lo:56 * k + hi], T.psa[:, 512 * b:512 * b + hi - lo],
+                                            MID, None, OP.add))
+
+    pw("sv", v_og[0])
+    turn(0)
+    pw("sv", v_og[1])
+    for j in (1, 2, 3):
+        turn(j)
 
     def numbers(lo, hi):
         vw("sg", g_kt)
+        vw("sv", v_nu)
         return inc("sv", V.tensor_copy(T.on[:, 16 * lo:16 * hi], T.kt[:, 0:KW].indirect(T.nu[:, lo:hi])))
 
     def near_lists(x, done):
         yw("sv", done)
         for k in range(4):
-            SY.dma_start(T.nl[:, 256 * k + 128 * x:256 * k + 128 * x + 128],
-                         T.on[32 * k:32 * k + 32:4, P * x:P * x + P]).then_inc(T.sem["dm%d" % (2 * k + x)], 16)
+            SY.dma_start(T.nl[:, 256 * k + cut * x:256 * k + cut * x + PARTS[x]],
+                         T.on[32 * k:32 * k + 32:4, 16 * cut * x:16 * (cut * x + PARTS[x])]
+                         ).then_inc(T.sem["dm%d" % (2 * k + x)], 16)
         SY.sem_inc(T.sem.sy, 1)
 
     def ghosts(on_vector, k, lo, hi):
@@ -265,6 +259,7 @@ def rank_program(g, core, T, topo):
         dst = T["gb%d" % k][:, 16 * lo:16 * hi]
         w = vw if on_vector else sw
         w("dx%d" % k, 128)
+        w("ss", s_z)
         w("sv", v_gl[k])
         return ("sv", inc("sv", V.tensor_copy(dst, src))) if on_vector else ("ss", inc("ss", S.activation(dst, src, COPY)))
 
@@ -286,31 +281,44 @@ def rank_program(g, core, T, topo):
             sent[0] += len(eng)
         g.remote_dma_fused(tr, local_sem=T.sem.sent)
 
-    numbers(0, 24)
     give_list(0)
-    for call in sends(rank, cores, topo):
-        lo, hi = 8 * min(d - 1 for d, c, e in call), 8 * max(d for d, c, e in call)
-        mid = (lo + hi) // 2
-        send(0, call, [ghosts(True, 0, lo, mid), ghosts(False, 0, mid, hi)])
-    for k in (1, 2, 3):
-        give_list(k)
-    near_lists(0, numbers(24, 128))
-    load_x(SY, 3, 0)
-    near_lists(1, numbers(128, 256))
+    send(0, first[0], [ghosts(False, 0, *spans[0])])
+    pw("sv", v_gl[0])
+    turn(4)
+    for k in range(4):
+        v_trr = inc("sv", V.tensor_copy(T.trr[:, k::4], T.psy[:, 512 * k:512 * k + 32]))
+    give_list(1)
+    send(0, first[1], [ghosts(False, 0, *spans[1])])
+
+    def stationary(rows):
+        for r in rows:
+            lo = 64 * (r // 16) + r % 16
+            hi = 64 * (r // 16) + 64
+            SY.dma_start(T.lt[lo:hi:16, 128 * r:128 * r + 128], T.trr[lo:hi:16, :]).then_inc(T.sem.dl, 16)
+
+    yw("sv", v_trr)
+    yw("ss", s_lt)
+    stationary(range(0, LS))
+    numbers(0, 32)
+    give_list(2)
+    numbers(32, 64)
+    give_list(3)
+    give_list(4)
+    near_lists(0, numbers(64, cut))
+    stationary(range(LS, 32))
+    yw("sv", numbers(cut, cut + 56))
     load_x(SY, 3, 1)
-    for k, rows in ((1, range(10, 16)), (2, range(16, 28))):
-        hand_on(k, [ghosts(False, k, 0, 56)])
-        send(k, own, [("sy", k)])
-        stationary(False, rows)
-    stationary(True, range(28, 32))
+    near_lists(1, numbers(cut + 56, 256))
+    for k in (1, 2):
+        hand_on(k, [ghosts(False, k, 0, 56), ("sy", 2 * k - 2)])
+        send(k, own, [("sy", 2)])
 
     arrive = [0, 0]
     for q in range(N):
         theirs, their_hands = relays(q, cores, topo)
         arrive[0] += sum(len(e) for call in sends(q, cores, topo) for d, c, e in call if c == core)
         arrive[1] += sum(len(e) for call in [theirs] + [x[2] for x in their_hands] for d, c, e in call if c == core)
-    pw("sv", last_lt["sv"])
-    pw("ss", last_lt["ss"])
+    pw("dl", 16 * 32)
     copied = {}
 
     def bank(n):
@@ -328,38 +336,43 @@ def rank_program(g, core, T, topo):
             yw(name, n)
         SY.dma_start(T.y[32 * k:32 * k + 32, :], T.o[:, 512 * k:512 * k + 512]).then_inc(T.sem.dy, 16)
 
-    pend = []
-    for n, (k, x) in enumerate(UNITS):
+    def copy_out(k, jobs):
+        copied.setdefault(k, []).extend(evac(*job) for job in jobs)
+        left[k] -= 1
+        if not left[k]:
+            store(k)
+
+    left = {k: sum(u[0] == k for u in UNITS) for k in range(4)}
+    pend, nb = [], 0
+    for n, (k, x, lo, mid, hi, by) in enumerate(UNITS):
         win = T["xb%d" % k][:, 0:BW]
         v = T["v%d" % n]
-        ps, col = bank(n)
-        base = 256 * k + 128 * x
-        if n == 2:
-            hand_on(3, [ghosts(True, 3, 0, 28), ghosts(False, 3, 28, 56)])
+        base, wide, dst = 256 * k + cut * x, hi - lo, 512 * k + 2 * cut * x + lo
+        if n == 1:
+            hand_on(3, [ghosts(True, 3, 0, GV), ghosts(False, 3, GV, 56)])
             send(3, own, [])
         for w in (vw, sw):
             w("arr%d" % k, arrive[min(k, 1)])
             w("dm%d" % (2 * k + x), 16)
             w("dx%d" % k, 128)
-        last = n == len(UNITS) - 1
-        for lo, hi in ([(0, 64), (64, 128)] if last else [(0, 128)]):
-            mid = (lo + hi) // 2
-            pw("sv", inc("sv", V.tensor_copy(v[:, 16 * lo:16 * mid], win.indirect(T.nl[:, base + lo:base + mid]))))
-            pw("ss", inc("ss", S.activation(v[:, 16 * mid:16 * hi], win.indirect(T.nl[:, base + mid:base + hi]), COPY)))
-            p_e = []
-            for e in range(2):
-                out = T.psa[:, lo:hi] if last and e else ps[:, col + 128 * e + lo:col + 128 * e + hi]
-                for d in range(8):
-                    p_y = inc("sp", PE.matmul(out, T.lt[:, 4 * d + k::32], v[:, 16 * lo + 2 * d + e:16 * hi:16], d == 0, d == 7))
-                p_e.append(p_y)
-            if len(pend) == 2 or last:
-                pn, pk, px, pp = pend.pop(0)
-                copied.setdefault(pk, []).append(evac(pn % 2 == 1, bank(pn)[0], bank(pn)[1], 256, 512 * pk + 256 * px, pp))
-                if px:
-                    store(pk)
-        pend.append((n, k, x, p_y))
-    copied[k].append(evac(True, ps, col, 128, 512 * k + 256 * x, p_e[0]))
-    copied[k].append(evac(False, T.psa, 0, 128, 512 * k + 256 * x + 128, p_e[1]))
-    store(k)
+            w("ss", s_z)
+        pw("sv", inc("sv", V.tensor_copy(v[:, 0:16 * (mid - lo)], win.indirect(T.nl[:, base + lo:base + mid]))))
+        pw("ss", inc("ss", S.activation(v[:, 16 * (mid - lo):16 * wide], win.indirect(T.nl[:, base + mid:base + hi]), COPY)))
+        jobs = []
+        for e in range(2):
+            ps, col = bank((nb + e * (len(by) - 1)) % 8)
+            col += wide * e
+            for d in range(8):
+                p_y = inc("sp", PE.matmul(ps[:, col:col + wide], T.lt[:, 4 * d + k::32], v[:, 2 * d + e:16 * wide:16],
+                                          d == 0, d == 7))
+            jobs.append((by[-e] == "V", ps, col, wide, dst + PARTS[x] * e, p_y))
+        if len(by) == 1:
+            jobs = [(by == "V", ps, col - wide, 2 * wide, dst, p_y)]
+        nb += len(by)
+        if len(pend) == 2:
+            copy_out(*pend.pop(0))
+        pend.append((k, jobs))
+    for job in pend:
+        copy_out(*job)
     SY.wait_ge(T.sem.dy, 64)
     g.wait_ge(T.sem.sent, sent[0])

from concourse.bass import DstId, RemoteDMATransfer
from concourse.mybir import dt, AluOpType, AxisListType, ActivationFunctionType

OP = AluOpType
COPY = ActivationFunctionType.Copy
N, P, E, M, G = 8, 2048, 4096, 512, 128
DX, DY = (-1, 0, 1, -1, 1, -1, 0, 1), (-1, -1, -1, 0, 0, 1, 1, 1)
FAR = [[(d, s) for d in range(8) for s in range(4)
        if max(abs(2 * DX[d] + s % 2 - c % 2), abs(2 * DY[d] + s // 2 - c // 2)) > 1] for c in range(4)]
Z = P + (N - 1) * G
XW = E + 16
GW = (N - 1) * G
BW = XW + GW
KW = Z + 16
KV = 1408
PARTS = (144, 112)
LS = 26
GV = 24
MID = E // 2

SCRATCH = {
    "kt": ("sbuf", [128, KW], "int32"),
    "ni": ("sbuf", [128, 8, 32], "int32"), "gi": ("sbuf", [128, 56], "int32"),
    "nu": ("sbuf", [128, 256], "uint16"), "gu": ("sbuf", [128, 56], "uint16"),
    "og": ("sbuf", [128, GW], "float16"), "on": ("sbuf", [128, 4096], "uint16"),
    "gl": ("sbuf", [128, 224], "uint16"), "nl": ("sbuf", [128, 1024], "uint16"),
    "im": ("sbuf", [128, 32], "int32"), "i16": ("sbuf", [128, 32], "int32"), "i32": ("sbuf", [128, 32], "int32"),
    "il": ("sbuf", [128, 144], "int32"), "i128": ("sbuf", [128, 144], "int32"), "sl": ("sbuf", [128, 144], "float16"),
    "rm": ("sbuf", [128, 32], "float32"), "em": ("sbuf", [128, 176], "bfloat16"),
    "tri": ("sbuf", [128, 108], "bfloat16"), "trf": ("sbuf", [128, 128], "bfloat16"),
    "trr": ("sbuf", [128, 128], "bfloat16"), "lt": ("sbuf", [128, 4096], "bfloat16"),
    "o": ("sbuf", [128, 2048], "float32"),
    "psy": ("psum", [128, 2048], "float32"), "psa": ("psum", [128, 2048], "float32"),
}
for _n in range(9):
    SCRATCH["v%d" % _n] = ("sbuf", [128, 16 * max(PARTS)], "bfloat16")
for _k in range(4):
    SCRATCH["xb%d" % _k] = ("sbuf", [128, BW], "bfloat16")
    SCRATCH["gb%d" % _k] = ("sbuf", [128, GW], "bfloat16")
SEMAPHORES = (["sy", "dl", "sv", "ss", "sp", "sg", "sent", "dk", "dg", "dn", "dt", "dy"] + ["arr%d" % k for k in range(4)]
              + ["hop%d" % k for k in range(1, 4)] + ["dx%d" % k for k in range(4)] + ["dm%d" % k for k in range(8)])
UNITS = [(0, 0, 0, 58, 144, "V"), (0, 1, 0, 52, 112, "V"), (1, 0, 0, 66, 144, "V"), (1, 1, 0, 52, 112, "V"),
         (2, 0, 0, 66, 144, "V"), (2, 1, 0, 52, 112, "V"), (3, 1, 0, 52, 112, "V"),
         (3, 0, 0, 36, 80, "VV"), (3, 0, 80, 110, 144, "VV")]


def sends(q, cores, topo):
    me = cores[q]
    dst = {d: cores[(q + d) % N] for d in range(1, N)}
    home = [d for d in dst if topo.chip(dst[d]) == topo.chip(me)]
    first = next(r for r in (range(1, 5), range(4, N)) if not set(r) & set(home))
    calls = []
    for group in (list(first), [d for d in dst if d not in first and d not in home]):
        call = []
        for j, d in enumerate(group):
            eng = topo.engines(me, dst[d])
            n = len(eng) // len(group)
            call.append((d, dst[d], eng[n * j:n * j + n]))
        calls.append(call)
    used = set(topo.engines(me, dst[first[0]]))
    for d in home:
        calls[1].append((d, dst[d], [e for e in topo.engines(me, dst[d]) if e not in used][::2]))
    return calls


def shared(eng, n):
    return [eng[len(eng) // n * j:len(eng) // n * (j + 1)] for j in range(n)]


def relays(q, cores, topo):
    me = cores[q]
    dst = {d: cores[(q + d) % N] for d in range(1, N)}
    kinds = {"home": [], "mate": [], "plane": [], "far": []}
    for d in dst:
        a, b = topo.chip(me), topo.chip(dst[d])
        kinds["home" if a == b else "mate" if topo.mates(a, b) else "plane" if topo.same_plane(a, b) else "far"].append(d)
    off = topo.engines(me, dst[kinds["far"][0]])
    inner = [e for e in topo.engines(me, dst[kinds["home"][0]]) if e not in off]
    own = [(d, dst[d], e) for d, e in zip(kinds["far"], shared(off, 2))] + [(d, dst[d], inner) for d in kinds["home"]]
    free = [c for c in topo.cores_of(me) if c not in cores and topo.die(c) == topo.die(me)]
    hands = []
    for kind, eng in zip(("mate", "plane"), shared(inner, 2)):
        h = next(c for c in free if topo.may_write(c, dst[kinds[kind][0]]))
        free.remove(h)
        hands.append((h, eng, [(d, dst[d], e) for d, e in zip(kinds[kind], shared(topo.engines(h, dst[kinds[kind][0]]), 2))]))
    return own, hands


def transfer(T, topo, core, eng, sem, src, dst):
    ad = topo.addr(core)
    return RemoteDMATransfer(dst_ids=[DstId(rid=ad[0], pnc=ad[1])], dma_engine_mask=sum(1 << e for e in eng),
                             remote_sem=T.sem[sem], src=src, dst=dst)


def to_ranks(g, T, topo, k, call):
    g.remote_dma_fused([transfer(T, topo, c, eng, "arr%d" % k, T["gb%d" % k][:, G * (d - 1):G * d],
                                 T["xb%d" % k][:, XW + G * (d - 1):XW + G * d]) for d, c, eng in call], local_sem=T.sem.sent)
    return sum(len(eng) for d, c, eng in call)


def helper_program(g, core, T, topo):
    cores = list(T.cores)
    for q in range(N):
        for h, eng, call in relays(q, cores, topo)[1]:
            if h == core:
                sent = 0
                for k in (1, 2, 3):
                    g.wait_ge(T.sem["hop%d" % k], len(eng))
                    sent += to_ranks(g, T, topo, k, call)
                g.wait_ge(T.sem.sent, sent)


def runs():
    pos = [32 * c + 4 * d + s for c in range(4) for d, s in FAR[c]]
    out, i = [], 0
    while i < len(pos):
        j = i
        while j + 1 < len(pos) and pos[j + 1] == pos[j] + 1:
            j += 1
        out.append((pos[i], i, j + 1 - i))
        i = j + 1
    return out


def rank_program(g, core, T, topo):
    rank = T.rank_of(core)
    if rank is None:
        return helper_program(g, core, T, topo)
    cores = list(T.cores)
    V, S, PE, SY = g.vector, g.scalar, g.tensor, g.sync
    cnt = {"sv": 0, "ss": 0, "sp": 0, "sg": 0}
    seen = {}

    def inc(name, op):
        op.then_inc(T.sem[name], 1)
        cnt[name] += 1
        return cnt[name]

    def wait(qn, q, name, n):
        if seen.get((qn, name), 0) < n:
            q.wait_ge(T.sem[name], n)
            seen[(qn, name)] = n

    def vw(name, n):
        wait("V", V, name, n)

    def sw(name, n):
        wait("S", S, name, n)

    def pw(name, n):
        wait("P", PE, name, n)

    def yw(name, n):
        wait("Y", SY, name, n)

    def load_x(q, k, w):
        for s in range(4):
            q.dma_start(T["xb%d" % k][64 * w + 16 * s:64 * w + 16 * s + 16, 0:E],
                        T.ex[32 * k + 16 * w:32 * k + 16 * w + 16, :]).then_inc(T.sem["dx%d" % k], 16)

    def iota(out, pattern, base, mult, **kw):
        wait("G", g, "sg", cnt["sg"])
        return inc("sg", g.iota(out, pattern, base, mult, **kw))

    m_lt = inc("sv", V.memset(T.lt[:, 0:512], 0.0))
    m_k = inc("sv", V.memset(T.kt[:, 0:KV], MID))
    g_k = iota(T.kt[:, KV:P], [[0, P - KV]], MID, 0)
    inc("sv", V.memset(T.lt[:, 3072:4096], 0.0))
    inc("sv", V.memset(T.em[:], 0.0))
    inc("sv", V.memset(T.trf[:], 0.0))
    g_im = iota(T.im[:], [[-1, 32]], 128, 1)
    g_il = iota(T.il[:], [[-1, 144]], 143, 4)
    iota(T.kt[:, P:Z], [[1, GW]], XW, 0)
    g_kt = iota(T.kt[:, Z:KW], [[0, KW - Z]], E, 0)
    vw("sg", g_im)
    a = inc("sv", V.tensor_scalar(T.i32[:], T.im[:], 31, None, OP.bitwise_and))
    vw("dg", 16)
    v_gu = inc("sv", V.tensor_copy(T.gu[:], T.gi[:]))
    vw("sv", a)
    for w in range(2):
        v_em = inc("sv", V.tensor_scalar(T.em[:, 48 + 64 * w:64 + 64 * w], T.i32[:, 16 * w:16 * w + 16], 0, None, OP.is_equal))
    vw("sg", g_il)
    vw("sv", inc("sv", V.tensor_scalar(T.i128[:], T.il[:], 127, None, OP.bitwise_and)))
    inc("sv", V.tensor_scalar(T.sl[:], T.i128[:], 0, None, OP.is_equal))

    SY.dma_start(T.gi[:], T.give[:]).then_inc(T.sem.dg, 16)
    S.dma_start(T.tri[:], T.tr[:]).then_inc(T.sem.dt, 16)
    S.dma_start(T.ni[:], T.near[:]).then_inc(T.sem.dn, 16)
    load_x(SY, 0, 0)
    yw("sv", m_k)
    yw("sg", g_k)
    SY.dma_start(T.kt[0:128:4, 0:P], T.kid[:]).then_inc(T.sem.dk, 16)
    load_x(SY, 0, 1)
    for k, w in ((1, 0), (1, 1), (2, 0), (2, 1), (3, 0)):
        load_x(SY, k, w)

    sw("sv", m_lt)
    sw("ss", inc("ss", S.activation(T.lt[:, 512:1024], T.lt[:, 0:512], COPY)))
    inc("ss", S.activation(T.lt[:, 1024:2048], T.lt[:, 0:1024], COPY))
    for k in range(4):
        s_z = inc("ss", S.activation(T["xb%d" % k][:, E:XW], T.lt[:, 0:XW - E], COPY))
    s_lt = inc("ss", S.activation(T.lt[:, 2048:3072], T.lt[:, 0:1024], COPY))
    vw("dt", 16)
    for pos, i, n in runs():
        v_trf = inc("sv", V.tensor_copy(T.trf[:, pos:pos + n], T.tri[:, i:i + n]))
    pw("sv", v_trf)
    for k in range(4):
        for s in range(4):
            p_t = inc("sp", PE.matmul(T.psy[:, 512 * k:512 * k + 32], T.em[32 * k:32 * k + 32, 48 - 16 * s:176 - 16 * s],
                                      T.trf[32 * k:32 * k + 32, s::4], s == 0, s == 3))
    cut = PARTS[0]

    vw("dk", 16)
    vw("sv", v_gu)
    first = sends(rank, cores, topo)
    spans = [(8 * min(d - 1 for d, c, e in call), 8 * max(d for d, c, e in call)) for call in first]
    v_og = [inc("sv", V.tensor_scalar(T.og[:, 16 * lo:16 * hi], T.kt[:, 0:P].indirect(T.gu[:, lo:hi]), -MID, None, OP.add))
            for lo, hi in spans]
    vw("dn", 16)
    inc("sv", V.tensor_copy(T.nu[:, 0:cut], T.ni[:, :, 0:cut // 8]))
    v_nu = inc("sv", V.tensor_copy(T.nu[:, cut:256], T.ni[:, :, cut // 8:32]))

    jobs = [(0, 0) + spans[0], (0, 3) + spans[1], (1, 1, 0, 56), (2, 2, 0, 56), (3, 0, 0, 56)]
    p_g, v_gl = {}, {}

    def turn(j):
        k, b, lo, hi = jobs[j]
        for a in range(16):
            p_g[j] = inc("sp", PE.matmul(T.psa[:, 512 * b:512 * b + hi - lo], T.sl[32 * k:32 * k + 32, 15 - a:143 - a],
                                         T.og[32 * k:32 * k + 32, 16 * lo + a:16 * hi:16], a == 0, a == 15))

    def give_list(j):
        k, b, lo, hi = jobs[j]
        vw("sp", p_g[j])
        v_gl[k] = inc("sv", V.tensor_scalar(T.gl[:, 56 * k + lo:56 * k + hi], T.psa[:, 512 * b:512 * b + hi - lo],
                                            MID, None, OP.add))

    pw("sv", v_og[0])
    turn(0)
    pw("sv", v_og[1])
    for j in (1, 2, 3):
        turn(j)

    def numbers(lo, hi):
        vw("sg", g_kt)
        vw("sv", v_nu)
        return inc("sv", V.tensor_copy(T.on[:, 16 * lo:16 * hi], T.kt[:, 0:KW].indirect(T.nu[:, lo:hi])))

    def near_lists(x, done):
        yw("sv", done)
        for k in range(4):
            SY.dma_start(T.nl[:, 256 * k + cut * x:256 * k + cut * x + PARTS[x]],
                         T.on[32 * k:32 * k + 32:4, 16 * cut * x:16 * (cut * x + PARTS[x])]
                         ).then_inc(T.sem["dm%d" % (2 * k + x)], 16)
        SY.sem_inc(T.sem.sy, 1)

    def ghosts(on_vector, k, lo, hi):
        src = T["xb%d" % k][:, 0:XW].indirect(T.gl[:, 56 * k + lo:56 * k + hi])
        dst = T["gb%d" % k][:, 16 * lo:16 * hi]
        w = vw if on_vector else sw
        w("dx%d" % k, 128)
        w("ss", s_z)
        w("sv", v_gl[k])
        return ("sv", inc("sv", V.tensor_copy(dst, src))) if on_vector else ("ss", inc("ss", S.activation(dst, src, COPY)))

    own, hands = relays(rank, cores, topo)
    sent = [0]

    def send(k, call, ready):
        for name, n in ready:
            wait("G", g, name, n)
        sent[0] += to_ranks(g, T, topo, k, call)

    def hand_on(k, ready):
        for name, n in ready:
            wait("G", g, name, n)
        tr = []
        for h, eng, call in hands:
            lo = G * (min(d for d, c, e in call) - 1)
            tr.append(transfer(T, topo, h, eng, "hop%d" % k, T["gb%d" % k][:, lo:lo + 2 * G], T["gb%d" % k][:, lo:lo + 2 * G]))
            sent[0] += len(eng)
        g.remote_dma_fused(tr, local_sem=T.sem.sent)

    give_list(0)
    send(0, first[0], [ghosts(False, 0, *spans[0])])
    pw("sv", v_gl[0])
    turn(4)
    for k in range(4):
        v_trr = inc("sv", V.tensor_copy(T.trr[:, k::4], T.psy[:, 512 * k:512 * k + 32]))
    give_list(1)
    send(0, first[1], [ghosts(False, 0, *spans[1])])

    def stationary(rows):
        for r in rows:
            lo = 64 * (r // 16) + r % 16
            hi = 64 * (r // 16) + 64
            SY.dma_start(T.lt[lo:hi:16, 128 * r:128 * r + 128], T.trr[lo:hi:16, :]).then_inc(T.sem.dl, 16)

    yw("sv", v_trr)
    yw("ss", s_lt)
    stationary(range(0, LS))
    numbers(0, 32)
    give_list(2)
    numbers(32, 64)
    give_list(3)
    give_list(4)
    near_lists(0, numbers(64, cut))
    stationary(range(LS, 32))
    yw("sv", numbers(cut, cut + 56))
    load_x(SY, 3, 1)
    near_lists(1, numbers(cut + 56, 256))
    for k in (1, 2):
        hand_on(k, [ghosts(False, k, 0, 56), ("sy", 2 * k - 2)])
        send(k, own, [("sy", 2)])

    arrive = [0, 0]
    for q in range(N):
        theirs, their_hands = relays(q, cores, topo)
        arrive[0] += sum(len(e) for call in sends(q, cores, topo) for d, c, e in call if c == core)
        arrive[1] += sum(len(e) for call in [theirs] + [x[2] for x in their_hands] for d, c, e in call if c == core)
    pw("dl", 16 * 32)
    copied = {}

    def bank(n):
        return (T.psa, 512 * n) if n < 4 else (T.psy, 512 * (n - 4))

    def evac(on_vector, ps, col, n, dst, p):
        if on_vector:
            vw("sp", p)
            return "sv", inc("sv", V.tensor_copy(T.o[:, dst:dst + n], ps[:, col:col + n]))
        sw("sp", p)
        return "ss", inc("ss", S.activation(T.o[:, dst:dst + n], ps[:, col:col + n], COPY))

    def store(k):
        for name, n in copied[k]:
            yw(name, n)
        SY.dma_start(T.y[32 * k:32 * k + 32, :], T.o[:, 512 * k:512 * k + 512]).then_inc(T.sem.dy, 16)

    def copy_out(k, jobs):
        copied.setdefault(k, []).extend(evac(*job) for job in jobs)
        left[k] -= 1
        if not left[k]:
            store(k)

    left = {k: sum(u[0] == k for u in UNITS) for k in range(4)}
    pend, nb = [], 0
    for n, (k, x, lo, mid, hi, by) in enumerate(UNITS):
        win = T["xb%d" % k][:, 0:BW]
        v = T["v%d" % n]
        base, wide, dst = 256 * k + cut * x, hi - lo, 512 * k + 2 * cut * x + lo
        if n == 1:
            hand_on(3, [ghosts(True, 3, 0, GV), ghosts(False, 3, GV, 56)])
            send(3, own, [])
        for w in (vw, sw):
            w("arr%d" % k, arrive[min(k, 1)])
            w("dm%d" % (2 * k + x), 16)
            w("dx%d" % k, 128)
            w("ss", s_z)
        pw("sv", inc("sv", V.tensor_copy(v[:, 0:16 * (mid - lo)], win.indirect(T.nl[:, base + lo:base + mid]))))
        pw("ss", inc("ss", S.activation(v[:, 16 * (mid - lo):16 * wide], win.indirect(T.nl[:, base + mid:base + hi]), COPY)))
        jobs = []
        for e in range(2):
            ps, col = bank((nb + e * (len(by) - 1)) % 8)
            col += wide * e
            for d in range(8):
                p_y = inc("sp", PE.matmul(ps[:, col:col + wide], T.lt[:, 4 * d + k::32], v[:, 2 * d + e:16 * wide:16],
                                          d == 0, d == 7))
            jobs.append((by[-e] == "V", ps, col, wide, dst + PARTS[x] * e, p_y))
        if len(by) == 1:
            jobs = [(by == "V", ps, col - wide, 2 * wide, dst, p_y)]
        nb += len(by)
        if len(pend) == 2:
            copy_out(*pend.pop(0))
        pend.append((k, jobs))
    for job in pend:
        copy_out(*job)
    SY.wait_ge(T.sem.dy, 64)
    g.wait_ge(T.sem.sent, sent[0])
